import numpy as np
import ml_dtypes


def mxq(x, axis, fmt="e4m3"):
    dtype, down = {"e4m3": (ml_dtypes.float8_e4m3fn, 7), "e5m2": (ml_dtypes.float8_e5m2, 14)}[fmt]
    v = np.moveaxis(np.asarray(x, np.float32).astype(ml_dtypes.bfloat16).astype(np.float64), axis, -1)
    blocks = v.reshape(v.shape[:-1] + (-1, 32))
    amax = np.abs(blocks).max(-1, keepdims=True)
    byte = np.maximum(np.where(amax > 0, np.frexp(amax)[1] - 1 + 127, 0) - down, 1)
    scale = np.exp2(byte - 127.0)
    codes = (blocks / scale).astype(np.float32).astype(dtype).astype(np.float64)
    return np.moveaxis((codes * scale).reshape(v.shape), -1, axis)


WIDE = False


def mx_kscale(k):
    if not WIDE:
        return np.ones(k)
    levels = np.array([10, -10, 5, -5, 0])
    if k % 512:
        return np.exp2(np.random.permutation(np.resize(levels, k // 32))).repeat(32)
    a = np.empty((k // 512, 16))
    for p in range(k // 512):
        a[p, :8] = np.random.permutation(np.resize(levels, 8))
        for g in range(8):
            far = levels[np.abs(levels - a[p, g]) >= 10]
            a[p, g + 8] = far[np.random.randint(len(far))]
    return np.exp2(a.ravel()).repeat(32)


def f64(x):
    return np.asarray(x).astype(np.float64)


def striped(idx):
    return np.tile(idx.reshape(-1, 16).T, (8, 1)).astype(np.uint16)


def unstriped(offs):
    return offs[:16].T.reshape(-1).astype(np.int64)


E2M1 = np.array([0.0, 0.5, 1.0, 1.5, 2.0, 3.0, 4.0, 6.0, -0.0, -0.5, -1.0, -1.5, -2.0, -3.0, -4.0, -6.0])


def pack_weight(w, fmt):
    k, n = w.shape
    w = f64(np.asarray(w, np.float32).astype(ml_dtypes.bfloat16)).reshape(k // 32, 32, n)
    amax = np.abs(w).max(1)
    if fmt == "e4m3":
        byte = np.frexp(amax)[1] - 1 + 127 - 7
    else:
        mant, ex = np.frexp(amax / 6.0)
        byte = np.where(mant > 0.5, ex, ex - 1) + 127
    byte = np.clip(np.where(amax > 0, byte, 1), 1, 254)
    scaled = (w * np.exp2(127.0 - byte)[:, None, :]).reshape(k, n).astype(np.float32)
    by_word = np.ascontiguousarray(scaled.reshape(k // 512, 128, 4, n).transpose(0, 1, 3, 2))
    if fmt == "e4m3":
        words = by_word.astype(ml_dtypes.float8_e4m3fn).view(np.uint8)
    else:
        c = by_word.astype(ml_dtypes.float4_e2m1fn).view(np.uint8) & 0xF
        words = (c[..., 0::2] | (c[..., 1::2] << 4)).reshape(k // 512, 128, 2 * n)
    return np.ascontiguousarray(words), np.ascontiguousarray(byte.astype(np.uint8).reshape(k // 512, 16, n))


def unpack_weight(words, scales, fmt):
    g, _, n = scales.shape
    words = np.ascontiguousarray(words).reshape(g, 128, n, -1)
    if fmt == "e4m3":
        vals = words.view(ml_dtypes.float8_e4m3fn).astype(np.float64)
    else:
        nib = np.empty((g, 128, n, 4), np.uint8)
        nib[..., 0::2] = words & 0xF
        nib[..., 1::2] = words >> 4
        vals = E2M1[nib]
    vals = vals * np.repeat(np.exp2(scales.astype(np.float64) - 127.0), 8, axis=1)[..., None]
    return vals.transpose(0, 1, 3, 2).reshape(g * 512, n)


def gelu(v):
    return 0.5 * v * (1.0 + np.tanh(np.sqrt(2.0 / np.pi) * (v + 0.044715 * v**3)))


K, T, S, M, N = 1024, 2048, 1024, 512, 512

def setup_inputs():
    n = np.random.standard_normal
    s = mx_kscale(K)[:, None]
    u = mx_kscale(S)
    idx = np.random.permutation(T)[:S]
    x = n((K, M)) / s
    tab_words, tab_scales = pack_weight(n((K, T)) * s / np.sqrt(K), "e4m3")
    tab2_words, tab2_scales = pack_weight(n((K, T)) * s / np.sqrt(K), "e4m3")
    w4_words, w4_scales = pack_weight(0.5 * n((K, N)) * s / np.sqrt(K), "e2m1")
    wdT = n((N, T)) / np.sqrt(S)
    wdT[:, idx] /= u
    g = np.exp(0.3 * n(S)) * u
    return {"x": x.astype(np.float32), "tab_words": tab_words, "tab_scales": tab_scales,
            "tab2_words": tab2_words, "tab2_scales": tab2_scales,
            "w4_words": w4_words, "w4_scales": w4_scales,
            "wdT": wdT.astype(np.float32), "g": g.astype(np.float32), "offs": striped(idx)}

def reference(x, tab_words, tab_scales, tab2_words, tab2_scales, w4_words, w4_scales, wdT, g, offs):
    v = unpack_weight(tab_words, tab_scales, "e4m3")[:, unstriped(offs)]
    v2 = unpack_weight(tab2_words, tab2_scales, "e4m3")[:, unstriped(offs)]
    w4 = unpack_weight(w4_words, w4_scales, "e2m1")
    wd = f64(wdT)[:, unstriped(offs)]
    xq = mxq(f64(x), 0, "e4m3")
    a = v.T @ xq
    b = v2.T @ xq
    h = a * (1.0 / (1.0 + b * b)) * f64(g)[:, None]
    return mxq(wd, 1, "e4m3") @ mxq(h, 0, "e4m3") + w4.T @ xq

@@ -1,0 +1,291 @@
+from contextlib import ExitStack
+
+import concourse.mybir as mybir
+from concourse.masks import make_identity
+
+K, T, S, M, N = 1024, 2048, 1024, 512, 512
+FLOPS = 2 * (2 * K * S * M + S * N * M + K * N * M)
+
+F32 = mybir.dt.float32
+BF16 = mybir.dt.bfloat16
+I32 = mybir.dt.int32
+U32 = mybir.dt.uint32
+U16 = mybir.dt.uint16
+U8 = mybir.dt.uint8
+FP8X4 = mybir.dt.float8_e4m3fn_x4
+FP4X4 = mybir.dt.float4_e2m1fn_x4
+ACT = mybir.ActivationFunctionType
+MULT = mybir.AluOpType.mult
+
+P = 128
+HALF = 256
+CH = 128
+
+
+def tile_list_divisive_norm_patch_kernel(
+    tc, x, tab_words, tab_scales, tab2_words, tab2_scales, w4_words, w4_scales, wdT, g, offs, out
+):
+    nc = tc.nc
+    with ExitStack() as ctx:
+        keep = ctx.enter_context(tc.tile_pool(name="keep", bufs=1))
+        psum = ctx.enter_context(tc.psum_pool(name="psum", bufs=1))
+
+        def held(shape, dtype, name):
+            return keep.tile(shape, dtype, name=name, align_bytes=64)
+
+        offsets = held([P, S // 16], U16, "offsets")
+        nc.sync.dma_start(offsets[:], offs)
+
+        def load_words(words, a, name):
+            t = held([P, T], I32, name)
+            nc.sync.dma_start(t[:], words[a].rearrange("p n t -> p (n t)").bitcast(I32))
+            return t
+
+        def zero_plane(width, name, engine):
+            t = held([P, width], U8, name)
+            engine.memset(t[:].bitcast(I32), 0)
+            return t
+
+        def load_table_scales(plane, scales):
+            for q in range(4):
+                nc.sync.dma_start(
+                    plane[:].bitcast(I32)[32 * q : 32 * q + 8, :],
+                    scales.bitcast(I32)[:, 4 * q : 4 * q + 4, :],
+                )
+
+        def load_x(h, a):
+            t = held([P, 4, HALF], F32, "xraw%d%d" % (h, a))
+            nc.sync.dma_start(
+                t[:],
+                x[512 * a : 512 * (a + 1), HALF * h : HALF * (h + 1)].rearrange("(p j) m -> p j m", j=4),
+            )
+            return t
+
+        plane2 = held([P, T], U8, "plane2")
+        nc.gpsimd.memset(plane2[:].bitcast(I32)[:, 0 : T // 8], 0)
+        nc.vector.memset(plane2[:].bitcast(I32)[:, T // 8 : T // 4], 0)
+        plane1 = zero_plane(T, "plane1", nc.vector)
+        plane4 = zero_plane(2 * N, "plane4", nc.vector)
+        warm = held([P, 2], F32, "warm")
+        nc.vector.memset(warm[:, 0:1], 1.0)
+        nc.scalar.activation(warm[:, 1:2], warm[:, 0:1], ACT.Abs_reciprocal_sqrt)
+        ident = held([P, P], F32, "ident")
+        grows = held([P, P], F32, "grows")
+        nc.gpsimd.memset(grows[:], 0.0)
+        for b in range(2):
+            nc.gpsimd.dma_start(
+                grows[4 * b : 4 * b + 4, :].rearrange("t (q r) -> t q r", r=8),
+                g[512 * b : 512 * (b + 1)].rearrange("(q t r) -> t q r", t=4, r=8),
+            )
+        make_identity(nc, ident[:])
+
+        load_table_scales(plane2, tab2_scales)
+        load_table_scales(plane1, tab_scales)
+        xraw = {(0, a): load_x(0, a) for a in range(2)}
+        words2 = [load_words(tab2_words, a, "words2_%d" % a) for a in range(2)]
+        for a in range(2):
+            xraw[1, a] = load_x(1, a)
+        words1 = [load_words(tab_words, a, "words1_%d" % a) for a in range(2)]
+        wraw = []
+        for i in range(4):
+            t = held([P, T], F32, "wraw%d" % i)
+            nc.sync.dma_start(t[:], wdT[P * i : P * (i + 1), :])
+            wraw.append(t)
+        w4 = held([P, 2, 2 * N], U8, "w4")
+        nc.sync.dma_start(w4[:].bitcast(I32), w4_words.bitcast(I32).rearrange("a p c -> p a c"))
+        for q in range(4):
+            nc.sync.dma_start(
+                plane4[:].bitcast(I32)[32 * q : 32 * q + 4, :].rearrange("r (a n) -> r a n", a=2),
+                w4_scales.bitcast(I32)[:, 4 * q : 4 * q + 4, :].rearrange("a r n -> r a n"),
+            )
+
+        def gather_words(window, b, name):
+            t = held([P, 512], U32, name)
+            nc.vector.tensor_copy(
+                t[:].rearrange("p (t q r) -> p q t r", t=4, r=8),
+                window[:].bitcast(U32).indirect(offsets[:, 32 * b : 32 * (b + 1)]),
+            )
+            return t
+
+        def gather_scales(plane, name):
+            picked = held([P, S], U8, name + "_picked")
+            nc.vector.tensor_copy(picked[:], plane[:].indirect(offsets[:]))
+            dealt = held([P, S], U8, name + "_dealt")
+            nc.vector.tensor_copy(
+                dealt[:].bitcast(I32).rearrange("p (b t q w) -> p b t q w", b=2, t=4, w=2),
+                picked[:].bitcast(I32).rearrange("p (b q t w) -> p b t q w", b=2, t=4, w=2),
+            )
+            return dealt
+
+        def quantize(src, width, name):
+            codes = held([P, width], U32, name + "_codes")
+            scales = held([P, width], U8, name + "_scales")
+            nc.vector.quantize_mx(out=codes[:].bitcast(FP8X4), scales=scales[:], in_=src)
+            return codes, scales
+
+        def quantize_x(h):
+            xg = held([P, 2, HALF, 4], BF16, "xg%d" % h)
+            for a in range(2):
+                nc.scalar.copy(
+                    xg[:, a].rearrange("p (c i) t -> p c t i", i=4),
+                    xraw[h, a][:].rearrange("p t (c i) -> p c t i", i=4),
+                )
+            return quantize(xg[:].rearrange("p a m t -> p (a m t)"), 2 * HALF, "xq%d" % h)
+
+        def first_product(dst, picked, dealt, b, t, xq, m0, width):
+            codes, scales = xq
+            for a in range(2):
+                cols = slice(HALF * a + m0, HALF * a + m0 + width)
+                nc.tensor.matmul_mx(
+                    out=dst,
+                    lhsT=picked[a][b][:, P * t : P * (t + 1)].bitcast(FP8X4),
+                    lhsT_scale=dealt[4 * a : P, 512 * b + P * t : 512 * b + P * (t + 1)],
+                    rhs=codes[:, cols].bitcast(FP8X4),
+                    rhs_scale=scales[:, cols],
+                    start=(a == 0),
+                    stop=(a == 1),
+                )
+
+        gbank = psum.tile([P, 4, P], F32, name="gbank", tag="tr", bufs=1)
+        nc.tensor.transpose(gbank[:, 0, :], grows[:], ident[:])
+        gcol = held([P, 8], F32, "gcol")
+        nc.scalar.copy(gcol[:], gbank[:, 0, 0:8])
+
+        picked2 = [[None, None], [None, None]]
+        picked1 = [[None, None], [None, None]]
+        dealt2 = gather_scales(plane2, "s2")
+        dealt1 = gather_scales(plane1, "s1")
+        xq = [quantize_x(0)]
+        picked2[0][0] = gather_words(words2[0], 0, "p2_00")
+        picked2[1][0] = gather_words(words2[1], 0, "p2_10")
+        picked2[0][1] = gather_words(words2[0], 1, "p2_01")
+        picked2[1][1] = gather_words(words2[1], 1, "p2_11")
+        xq.append(quantize_x(1))
+        for b in range(2):
+            for a in range(2):
+                picked1[a][b] = gather_words(words1[a], b, "p1_%d%d" % (a, b))
+        scratch = {}
+
+        def squares(b, h):
+            sq = held([P, 4 * HALF], F32, "sq%d%d" % (b, h))
+            for u in range(2):
+                bank = psum.tile([P, 2, HALF], F32, name="bbank", tag="b", bufs=2)
+                for e in range(2):
+                    first_product(bank[:, e, :], picked2, dealt2, b, 2 * u + e, xq[h], 0, HALF)
+                nc.scalar.activation(
+                    sq[:, 2 * HALF * u : 2 * HALF * (u + 1)], bank[:].rearrange("p e m -> p (e m)"), ACT.Square
+                )
+            return sq
+
+        def weights_of(b, h):
+            sq = squared[b, h]
+            root = held([P, 4 * HALF], F32, "root%d%d" % (b, h))
+            nc.scalar.activation(root[:], sq[:], ACT.Abs_reciprocal_sqrt, bias=1.0)
+            inv = held([P, 4 * HALF], F32, "inv%d%d" % (b, h))
+            nc.scalar.activation(inv[:], root[:], ACT.Square)
+            scratch[b, h] = (sq, root, inv)
+
+        def with_gain(b, h):
+            inv = scratch[b, h][2]
+            wg = held([P, 4, HALF], F32, "wg%d%d" % (b, h))
+            for t in range(4):
+                nc.scalar.activation(
+                    wg[:, t, :], inv[:, HALF * t : HALF * (t + 1)], ACT.Copy, scale=gcol[:, 4 * b + t : 4 * b + t + 1]
+                )
+            return wg
+
+        def responses(b, h, wg):
+            made = []
+            for c in range(2):
+                bank = psum.tile([P, 4, CH], F32, name="abank", tag="a", bufs=2)
+                for t in range(4):
+                    first_product(bank[:, t, :], picked1, dealt1, b, t, xq[h], CH * c, CH)
+                hg = held([P, CH, 4], BF16, "hg%d%d%d" % (b, h, c))
+                nc.vector.tensor_tensor(
+                    hg[:].rearrange("p (c i) t -> p c t i", i=4),
+                    bank[:].rearrange("p t (c i) -> p c t i", i=4),
+                    wg[:, :, CH * c : CH * (c + 1)].rearrange("p t (c i) -> p c t i", i=4),
+                    MULT,
+                )
+                made.append(hg)
+            return [
+                quantize(hg[:].rearrange("p m t -> p (m t)"), CH, "hq%d%d%d" % (b, h, c)) for c, hg in enumerate(made)
+            ]
+
+        def down_weights(i, room):
+            wb = held([P, S], BF16, "wb%d" % i)
+            nc.vector.tensor_copy(
+                wb[:].rearrange("p (u q r e) -> p q u e r", u=2, r=8, e=2),
+                wraw[i][:].indirect(offsets[:]),
+            )
+            bank = psum.tile([P, 4, P], F32, name="wbank", tag="b" if i % 2 else "tr", bufs=2 if i % 2 else 1)
+            for b in range(2):
+                for u in range(2):
+                    nc.tensor.transpose(
+                        bank[:, 2 * b + u, :], wb[:].bitcast(F32)[:, 256 * u + P * b : 256 * u + P * (b + 1)], ident[:]
+                    )
+            words = room[:, 0 : 4 * P]
+            nc.scalar.copy(
+                words.rearrange("p (b n u) -> p b n u", b=2, u=2),
+                bank[:].rearrange("p (b u) n -> p b n u", b=2),
+            )
+            return quantize(words.bitcast(BF16), 2 * P, "wq%d" % i)
+
+        hq = {}
+        wq = []
+        squared = {(b, h): squares(b, h) for h in range(2) for b in range(2)}
+        weights_of(0, 0)
+        hq[0, 0] = responses(0, 0, with_gain(0, 0))
+        weights_of(1, 0)
+        wq.append(down_weights(0, scratch[1, 0][0]))
+        gained = with_gain(1, 0)
+        wq.append(down_weights(1, scratch[1, 0][2]))
+        hq[1, 0] = responses(1, 0, gained)
+        weights_of(0, 1)
+        gained = with_gain(0, 1)
+        wq.append(down_weights(2, scratch[0, 1][2]))
+        hq[0, 1] = responses(0, 1, gained)
+        weights_of(1, 1)
+        wq.append(down_weights(3, scratch[1, 1][1]))
+        hq[1, 1] = responses(1, 1, with_gain(1, 1))
+
+        out_view = out.rearrange("(i p) m -> p i m", p=P)
+        for h in range(2):
+            for c in range(2):
+                last = (h, c) == (1, 1)
+                bank = psum.tile([P, 4, CH], F32, name="obank", tag="b" if last else "o", bufs=2 if last else 3)
+                xcodes, xscales = xq[h]
+                for i in range(4):
+                    for a in range(2):
+                        cols = slice(HALF * a + CH * c, HALF * a + CH * (c + 1))
+                        nc.tensor.matmul_mx(
+                            out=bank[:, i, :],
+                            lhsT=w4[:, a, 2 * P * i : 2 * P * (i + 1)].bitcast(FP4X4),
+                            lhsT_scale=plane4[:, N * a + P * i : N * a + P * (i + 1)],
+                            rhs=xcodes[:, cols].bitcast(FP8X4),
+                            rhs_scale=xscales[:, cols],
+                            start=(i == 0 and a == 0),
+                            stop=False,
+                        )
+                order = [(b, i) for b in range(2) for i in range(4)]
+                if h == 0:
+                    order = [(b, i) for i in range(4) for b in range(2)]
+                for b, i in order:
+                    hcodes, hscales = hq[b, h][c]
+                    wcodes, wscales = wq[i]
+                    nc.tensor.matmul_mx(
+                        out=bank[:, i, :],
+                        lhsT=wcodes[:, P * b : P * (b + 1)].bitcast(FP8X4),
+                        lhsT_scale=wscales[:, P * b : P * (b + 1)],
+                        rhs=hcodes[:].bitcast(FP8X4),
+                        rhs_scale=hscales[:],
+                        start=False,
+                        stop=(b == 1 and i == 3),
+                    )
+                res = held([P, 4, CH], F32, "res%d%d" % (h, c))
+                if last:
+                    nc.vector.tensor_copy(res[:], bank[:])
+                else:
+                    nc.scalar.copy(res[:], bank[:])
+                m0 = HALF * h + CH * c
+                nc.sync.dma_start(out_view[:, :, m0 : m0 + CH], res[:])

@@ -1,7 +1,6 @@
 from contextlib import ExitStack
 
 import concourse.mybir as mybir
-from concourse.masks import make_identity
 
 K, T, S, M, N = 1024, 2048, 1024, 512, 512
 FLOPS = 2 * (2 * K * S * M + S * N * M + K * N * M)
@@ -16,6 +15,7 @@ FP8X4 = mybir.dt.float8_e4m3fn_x4
 FP4X4 = mybir.dt.float4_e2m1fn_x4
 ACT = mybir.ActivationFunctionType
 MULT = mybir.AluOpType.mult
+ADD = mybir.AluOpType.add
 
 P = 128
 HALF = 256
@@ -69,43 +69,62 @@ def tile_list_divisive_norm_patch_kernel(
         warm = held([P, 2], F32, "warm")
         nc.vector.memset(warm[:, 0:1], 1.0)
         nc.scalar.activation(warm[:, 1:2], warm[:, 0:1], ACT.Abs_reciprocal_sqrt)
-        ident = held([P, P], F32, "ident")
-        grows = held([P, P], F32, "grows")
+        grows = held([P, 2 * P], F32, "grows")
         nc.gpsimd.memset(grows[:], 0.0)
-        for b in range(2):
-            nc.gpsimd.dma_start(
-                grows[4 * b : 4 * b + 4, :].rearrange("t (q r) -> t q r", r=8),
-                g[512 * b : 512 * (b + 1)].rearrange("(q t r) -> t q r", t=4, r=8),
-            )
-        make_identity(nc, ident[:])
-
-        load_table_scales(plane2, tab2_scales)
-        load_table_scales(plane1, tab_scales)
-        xraw = {(0, a): load_x(0, a) for a in range(2)}
-        words2 = [load_words(tab2_words, a, "words2_%d" % a) for a in range(2)]
-        for a in range(2):
-            xraw[1, a] = load_x(1, a)
-        words1 = [load_words(tab_words, a, "words1_%d" % a) for a in range(2)]
-        wraw = []
-        for i in range(4):
-            t = held([P, T], F32, "wraw%d" % i)
-            nc.sync.dma_start(t[:], wdT[P * i : P * (i + 1), :])
-            wraw.append(t)
-        w4 = held([P, 2, 2 * N], U8, "w4")
-        nc.sync.dma_start(w4[:].bitcast(I32), w4_words.bitcast(I32).rearrange("a p c -> p a c"))
+        nc.gpsimd.dma_start(
+            grows[0:4, :].rearrange("t (q r) -> t q r", r=8),
+            g.rearrange("(q t r) -> t q r", t=4, r=8),
+        )
+        ones = held([P, P], F32, "ones")
+        nc.vector.memset(ones[:], 1.0)
+        column = held([P, P], F32, "column")
+        nc.vector.tensor_tensor_scan(column[:], ones[:], ones[:], -1.0, MULT, ADD)
+        within = held([P, 32], F32, "within")
+        nc.vector.transpose(within[:], column[:, 0:32])
+        first = held([P, 1], F32, "first")
         for q in range(4):
-            nc.sync.dma_start(
+            nc.vector.memset(first[32 * q : 32 * (q + 1), :], float(32 * q))
+        ident = held([P, P], F32, "ident")
+        nc.vector.tensor_scalar(
+            ident[:], column[:], first[:], within[:, 0:1], mybir.AluOpType.subtract, mybir.AluOpType.is_equal
+        )
+
+        for q in range(4):
+            nc.gpsimd.dma_start(
                 plane4[:].bitcast(I32)[32 * q : 32 * q + 4, :].rearrange("r (a n) -> r a n", a=2),
                 w4_scales.bitcast(I32)[:, 4 * q : 4 * q + 4, :].rearrange("a r n -> r a n"),
             )
+        words2, words1, xraw, wraw = [], [], {}, []
+        w4 = held([P, 2, 2 * N], U8, "w4")
 
-        def gather_words(window, b, name):
-            t = held([P, 512], U32, name)
+        def load_down(i):
+            t = held([P, T], F32, "wraw%d" % i)
+            nc.sync.dma_start(t[:], wdT[P * i : P * (i + 1), :])
+            wraw.append(t)
+
+        load_table_scales(plane2, tab2_scales)
+        load_table_scales(plane1, tab_scales)
+        words2.append(load_words(tab2_words, 0, "words2_0"))
+        xraw[0, 0] = load_x(0, 0)
+        xraw[0, 1] = load_x(0, 1)
+        words2.append(load_words(tab2_words, 1, "words2_1"))
+        xraw[1, 0] = load_x(1, 0)
+        xraw[1, 1] = load_x(1, 1)
+        words1.append(load_words(tab_words, 0, "words1_0"))
+        words1.append(load_words(tab_words, 1, "words1_1"))
+        load_down(0)
+        load_down(1)
+        nc.sync.dma_start(w4[:].bitcast(I32), w4_words.bitcast(I32).rearrange("a p c -> p a c"))
+        load_down(2)
+        load_down(3)
+
+        def gather_words(window, b0, nb, name):
+            t = held([P, 4, nb, P], U32, name)
             nc.vector.tensor_copy(
-                t[:].rearrange("p (t q r) -> p q t r", t=4, r=8),
-                window[:].bitcast(U32).indirect(offsets[:, 32 * b : 32 * (b + 1)]),
+                t[:].rearrange("p t b (q r) -> p (b q) t r", r=8),
+                window[:].bitcast(U32).indirect(offsets[:, 32 * b0 : 32 * (b0 + nb)]),
             )
-            return t
+            return [t[:, :, b, :] for b in range(nb)]
 
         def gather_scales(plane, name):
             picked = held([P, S], U8, name + "_picked")
@@ -138,7 +157,7 @@ def tile_list_divisive_norm_patch_kernel(
                 cols = slice(HALF * a + m0, HALF * a + m0 + width)
                 nc.tensor.matmul_mx(
                     out=dst,
-                    lhsT=picked[a][b][:, P * t : P * (t + 1)].bitcast(FP8X4),
+                    lhsT=picked[a][b][:, t, :].bitcast(FP8X4),
                     lhsT_scale=dealt[4 * a : P, 512 * b + P * t : 512 * b + P * (t + 1)],
                     rhs=codes[:, cols].bitcast(FP8X4),
                     rhs_scale=scales[:, cols],
@@ -147,27 +166,33 @@ def tile_list_divisive_norm_patch_kernel(
                 )
 
         gbank = psum.tile([P, 4, P], F32, name="gbank", tag="tr", bufs=1)
-        nc.tensor.transpose(gbank[:, 0, :], grows[:], ident[:])
-        gcol = held([P, 8], F32, "gcol")
-        nc.scalar.copy(gcol[:], gbank[:, 0, 0:8])
+        for b in range(2):
+            nc.tensor.transpose(gbank[:, b, :], grows[:, P * b : P * (b + 1)], ident[:])
 
-        picked2 = [[None, None], [None, None]]
-        picked1 = [[None, None], [None, None]]
         dealt2 = gather_scales(plane2, "s2")
         dealt1 = gather_scales(plane1, "s1")
+        picked2 = [gather_words(words2[0], 0, 2, "p2_0")]
         xq = [quantize_x(0)]
-        picked2[0][0] = gather_words(words2[0], 0, "p2_00")
-        picked2[1][0] = gather_words(words2[1], 0, "p2_10")
-        picked2[0][1] = gather_words(words2[0], 1, "p2_01")
-        picked2[1][1] = gather_words(words2[1], 1, "p2_11")
+        picked2.append(gather_words(words2[1], 0, 1, "p2_10") + gather_words(words2[1], 1, 1, "p2_11"))
         xq.append(quantize_x(1))
-        for b in range(2):
-            for a in range(2):
-                picked1[a][b] = gather_words(words1[a], b, "p1_%d%d" % (a, b))
+        gcol = xraw[0, 1][:, 0, 0:8]
+        nc.scalar.copy(gcol.rearrange("p (b t) -> p b t", b=2), gbank[:, 0:2, 0:4])
+        picked1 = [gather_words(words1[a], 0, 2, "p1_%d" % a) for a in range(2)]
+        picked_down = []
+        for i in range(4):
+            wb = held([P, S], BF16, "wb%d" % i)
+            nc.vector.tensor_copy(
+                wb[:].rearrange("p (u q r e) -> p q u e r", u=2, r=8, e=2),
+                wraw[i][:].indirect(offsets[:]),
+            )
+            picked_down.append(wb)
         scratch = {}
 
         def squares(b, h):
-            sq = held([P, 4 * HALF], F32, "sq%d%d" % (b, h))
+            if (b, h) == (0, 0):
+                sq = xraw[1, 1][:].rearrange("p j m -> p (j m)")
+            else:
+                sq = held([P, 4 * HALF], F32, "sq%d%d" % (b, h))
             for u in range(2):
                 bank = psum.tile([P, 2, HALF], F32, name="bbank", tag="b", bufs=2)
                 for e in range(2):
@@ -180,7 +205,7 @@ def tile_list_divisive_norm_patch_kernel(
         def weights_of(b, h):
             sq = squared[b, h]
             root = held([P, 4 * HALF], F32, "root%d%d" % (b, h))
-            nc.scalar.activation(root[:], sq[:], ACT.Abs_reciprocal_sqrt, bias=1.0)
+            nc.scalar.activation(root[:], sq[:, :], ACT.Abs_reciprocal_sqrt, bias=1.0)
             inv = held([P, 4 * HALF], F32, "inv%d%d" % (b, h))
             nc.scalar.activation(inv[:], root[:], ACT.Square)
             scratch[b, h] = (sq, root, inv)
@@ -195,29 +220,26 @@ def tile_list_divisive_norm_patch_kernel(
             return wg
 
         def responses(b, h, wg):
-            made = []
+            hg = held([P, HALF, 4], BF16, "hg%d%d" % (b, h))
             for c in range(2):
                 bank = psum.tile([P, 4, CH], F32, name="abank", tag="a", bufs=2)
                 for t in range(4):
                     first_product(bank[:, t, :], picked1, dealt1, b, t, xq[h], CH * c, CH)
-                hg = held([P, CH, 4], BF16, "hg%d%d%d" % (b, h, c))
                 nc.vector.tensor_tensor(
-                    hg[:].rearrange("p (c i) t -> p c t i", i=4),
+                    hg[:, CH * c : CH * (c + 1), :].rearrange("p (c i) t -> p c t i", i=4),
                     bank[:].rearrange("p t (c i) -> p c t i", i=4),
                     wg[:, :, CH * c : CH * (c + 1)].rearrange("p t (c i) -> p c t i", i=4),
                     MULT,
                 )
-                made.append(hg)
-            return [
-                quantize(hg[:].rearrange("p m t -> p (m t)"), CH, "hq%d%d%d" % (b, h, c)) for c, hg in enumerate(made)
-            ]
+            flat = hg[:].rearrange("p m t -> p (m t)")
+            if (b, h) == (1, 1):
+                parts = [quantize(flat[:, 4 * CH * c : 4 * CH * (c + 1)], CH, "hq11%d" % c) for c in range(2)]
+                return [(codes[:, :], scales[:, :]) for codes, scales in parts]
+            codes, scales = quantize(flat, HALF, "hq%d%d" % (b, h))
+            return [(codes[:, CH * c : CH * (c + 1)], scales[:, CH * c : CH * (c + 1)]) for c in range(2)]
 
         def down_weights(i, room):
-            wb = held([P, S], BF16, "wb%d" % i)
-            nc.vector.tensor_copy(
-                wb[:].rearrange("p (u q r e) -> p q u e r", u=2, r=8, e=2),
-                wraw[i][:].indirect(offsets[:]),
-            )
+            wb = picked_down[i]
             bank = psum.tile([P, 4, P], F32, name="wbank", tag="b" if i % 2 else "tr", bufs=2 if i % 2 else 1)
             for b in range(2):
                 for u in range(2):
@@ -233,15 +255,16 @@ def tile_list_divisive_norm_patch_kernel(
 
         hq = {}
         wq = []
-        squared = {(b, h): squares(b, h) for h in range(2) for b in range(2)}
+        squared = {(b, 0): squares(b, 0) for b in range(2)}
         weights_of(0, 0)
         hq[0, 0] = responses(0, 0, with_gain(0, 0))
+        squared[0, 1] = squares(0, 1)
         weights_of(1, 0)
         wq.append(down_weights(0, scratch[1, 0][0]))
-        gained = with_gain(1, 0)
-        wq.append(down_weights(1, scratch[1, 0][2]))
-        hq[1, 0] = responses(1, 0, gained)
+        hq[1, 0] = responses(1, 0, with_gain(1, 0))
+        squared[1, 1] = squares(1, 1)
         weights_of(0, 1)
+        wq.append(down_weights(1, scratch[0, 1][0]))
         gained = with_gain(0, 1)
         wq.append(down_weights(2, scratch[0, 1][2]))
         hq[0, 1] = responses(0, 1, gained)
@@ -277,8 +300,8 @@ def tile_list_divisive_norm_patch_kernel(
                         out=bank[:, i, :],
                         lhsT=wcodes[:, P * b : P * (b + 1)].bitcast(FP8X4),
                         lhsT_scale=wscales[:, P * b : P * (b + 1)],
-                        rhs=hcodes[:].bitcast(FP8X4),
-                        rhs_scale=hscales[:],
+                        rhs=hcodes.bitcast(FP8X4),
+                        rhs_scale=hscales,
                         start=False,
                         stop=(b == 1 and i == 3),
                     )

@@ -30,8 +30,8 @@ def tile_list_divisive_norm_patch_kernel(
         keep = ctx.enter_context(tc.tile_pool(name="keep", bufs=1))
         psum = ctx.enter_context(tc.psum_pool(name="psum", bufs=1))
 
-        def held(shape, dtype, name):
-            return keep.tile(shape, dtype, name=name, align_bytes=64)
+        def held(shape, dtype, name, tag=""):
+            return keep.tile(shape, dtype, name=name, tag=tag or name, align_bytes=64)
 
         offsets = held([P, S // 16], U16, "offsets")
         nc.sync.dma_start(offsets[:], offs)
@@ -85,9 +85,9 @@ def tile_list_divisive_norm_patch_kernel(
         for q in range(4):
             nc.vector.memset(first[32 * q : 32 * (q + 1), :], float(32 * q))
         ident = held([P, P], F32, "ident")
-        nc.vector.tensor_scalar(
-            ident[:], column[:], first[:], within[:, 0:1], mybir.AluOpType.subtract, mybir.AluOpType.is_equal
-        )
+        row = held([P, 1], F32, "row")
+        nc.gpsimd.tensor_tensor(row[:], first[:], within[:, 0:1], ADD)
+        nc.gpsimd.tensor_scalar(ident[:], column[:], row[:], None, mybir.AluOpType.is_equal)
 
         for q in range(4):
             nc.gpsimd.dma_start(
@@ -136,8 +136,8 @@ def tile_list_divisive_norm_patch_kernel(
             )
             return dealt
 
-        def quantize(src, width, name):
-            codes = held([P, width], U32, name + "_codes")
+        def quantize(src, width, name, tag=""):
+            codes = held([P, width], U32, name + "_codes", tag)
             scales = held([P, width], U8, name + "_scales")
             nc.vector.quantize_mx(out=codes[:].bitcast(FP8X4), scales=scales[:], in_=src)
             return codes, scales
@@ -165,18 +165,13 @@ def tile_list_divisive_norm_patch_kernel(
                     stop=(a == 1),
                 )
 
-        gbank = psum.tile([P, 4, P], F32, name="gbank", tag="tr", bufs=1)
-        for b in range(2):
-            nc.tensor.transpose(gbank[:, b, :], grows[:, P * b : P * (b + 1)], ident[:])
-
         dealt2 = gather_scales(plane2, "s2")
         dealt1 = gather_scales(plane1, "s1")
         picked2 = [gather_words(words2[0], 0, 2, "p2_0")]
         xq = [quantize_x(0)]
         picked2.append(gather_words(words2[1], 0, 1, "p2_10") + gather_words(words2[1], 1, 1, "p2_11"))
         xq.append(quantize_x(1))
-        gcol = xraw[0, 1][:, 0, 0:8]
-        nc.scalar.copy(gcol.rearrange("p (b t) -> p b t", b=2), gbank[:, 0:2, 0:4])
+        gcol = held([P, 8], F32, "gcol")
         picked1 = [gather_words(words1[a], 0, 2, "p1_%d" % a) for a in range(2)]
         picked_down = []
         for i in range(4):
@@ -202,12 +197,14 @@ def tile_list_divisive_norm_patch_kernel(
                 )
             return sq
 
-        def weights_of(b, h):
+        def weights_of(b, h, square_root=True):
             sq = squared[b, h]
             root = held([P, 4 * HALF], F32, "root%d%d" % (b, h))
             nc.scalar.activation(root[:], sq[:, :], ACT.Abs_reciprocal_sqrt, bias=1.0)
-            inv = held([P, 4 * HALF], F32, "inv%d%d" % (b, h))
-            nc.scalar.activation(inv[:], root[:], ACT.Square)
+            inv = None
+            if square_root:
+                inv = held([P, 4 * HALF], F32, "inv%d%d" % (b, h))
+                nc.scalar.activation(inv[:], root[:], ACT.Square)
             scratch[b, h] = (sq, root, inv)
 
         def with_gain(b, h):
@@ -238,6 +235,60 @@ def tile_list_divisive_norm_patch_kernel(
             codes, scales = quantize(flat, HALF, "hq%d%d" % (b, h))
             return [(codes[:, CH * c : CH * (c + 1)], scales[:, CH * c : CH * (c + 1)]) for c in range(2)]
 
+        def turn_gain():
+            gbank = psum.tile([P, 2, P], F32, name="gbank", tag="b", bufs=2)
+            for b in range(2):
+                nc.tensor.transpose(gbank[:, b, :], grows[:, P * b : P * (b + 1)], ident[:])
+            nc.scalar.copy(gcol[:].rearrange("p (b t) -> p b t", b=2), gbank[:, :, 0:4])
+
+        def responses_aside(b, h):
+            inv = scratch[b, h][2][:].rearrange("p (t m) -> p t m", t=4)
+            drive = held([P, 4, HALF], F32, "drive%d%d" % (b, h))
+            for u in range(2):
+                bank = psum.tile([P, 2, HALF], F32, name="abank", tag="a", bufs=2)
+                for e in range(2):
+                    first_product(bank[:, e, :], picked1, dealt1, b, 2 * u + e, xq[h], 0, HALF)
+                for e in range(2):
+                    t = 2 * u + e
+                    nc.scalar.activation(
+                        drive[:, t, :], bank[:, e, :], ACT.Copy, scale=gcol[:, 4 * b + t : 4 * b + t + 1]
+                    )
+            hg = held([P, HALF, 4], BF16, "hg%d%d" % (b, h))
+            for c in range(2):
+                nc.gpsimd.tensor_tensor(
+                    hg[:, CH * c : CH * (c + 1), :].rearrange("p (c i) t -> p c t i", i=4),
+                    drive[:, :, CH * c : CH * (c + 1)].rearrange("p t (c i) -> p c t i", i=4),
+                    inv[:, :, CH * c : CH * (c + 1)].rearrange("p t (c i) -> p c t i", i=4),
+                    MULT,
+                )
+            return hg
+
+        def responses_twice(b, h, engine):
+            root = scratch[b, h][1][:].rearrange("p (t m) -> p t m", t=4)
+            once = held([P, 4, HALF], F32, "once%d%d" % (b, h))
+            for u in range(2):
+                bank = psum.tile([P, 2, HALF], F32, name="abank", tag="a", bufs=2)
+                for e in range(2):
+                    first_product(bank[:, e, :], picked1, dealt1, b, 2 * u + e, xq[h], 0, HALF)
+                for e in range(2):
+                    t = 2 * u + e
+                    nc.vector.scalar_tensor_tensor(
+                        once[:, t, :], bank[:, e, :], gcol[:, 4 * b + t : 4 * b + t + 1], root[:, t, :], MULT, MULT
+                    )
+            hg = held([P, HALF, 4], BF16, "hg%d%d" % (b, h))
+            for c in range(2):
+                engine.tensor_tensor(
+                    hg[:, CH * c : CH * (c + 1), :].rearrange("p (c i) t -> p c t i", i=4),
+                    once[:, :, CH * c : CH * (c + 1)].rearrange("p t (c i) -> p c t i", i=4),
+                    root[:, :, CH * c : CH * (c + 1)].rearrange("p t (c i) -> p c t i", i=4),
+                    MULT,
+                )
+            return hg
+
+        def quantize_h(hg, name, tag=""):
+            codes, scales = quantize(hg[:].rearrange("p m t -> p (m t)"), HALF, name, tag)
+            return [(codes[:, CH * c : CH * (c + 1)], scales[:, CH * c : CH * (c + 1)]) for c in range(2)]
+
         def down_weights(i, room):
             wb = picked_down[i]
             bank = psum.tile([P, 4, P], F32, name="wbank", tag="b" if i % 2 else "tr", bufs=2 if i % 2 else 1)
@@ -255,22 +306,26 @@ def tile_list_divisive_norm_patch_kernel(
 
         hq = {}
         wq = []
-        squared = {(b, 0): squares(b, 0) for b in range(2)}
+        squared = {(0, 0): squares(0, 0)}
+        turn_gain()
+        squared[1, 0] = squares(1, 0)
         weights_of(0, 0)
-        hq[0, 0] = responses(0, 0, with_gain(0, 0))
+        hg00 = responses_aside(0, 0)
         squared[0, 1] = squares(0, 1)
         weights_of(1, 0)
         wq.append(down_weights(0, scratch[1, 0][0]))
-        hq[1, 0] = responses(1, 0, with_gain(1, 0))
+        hg10 = responses_aside(1, 0)
         squared[1, 1] = squares(1, 1)
-        weights_of(0, 1)
+        weights_of(0, 1, True)
+        hq[0, 0] = quantize_h(hg00, "hq00", "root01")
         wq.append(down_weights(1, scratch[0, 1][0]))
-        gained = with_gain(0, 1)
-        wq.append(down_weights(2, scratch[0, 1][2]))
-        hq[0, 1] = responses(0, 1, gained)
+        hq[0, 1] = responses(0, 1, with_gain(0, 1))
         weights_of(1, 1)
-        wq.append(down_weights(3, scratch[1, 1][1]))
-        hq[1, 1] = responses(1, 1, with_gain(1, 1))
+        hq[1, 0] = quantize_h(hg10, "hq10", "root11")
+        wq.append(down_weights(2, scratch[1, 1][0]))
+        gained = with_gain(1, 1)
+        wq.append(down_weights(3, scratch[1, 1][2]))
+        hq[1, 1] = responses(1, 1, gained)
 
         out_view = out.rearrange("(i p) m -> p i m", p=P)
         for h in range(2):

from contextlib import ExitStack

import concourse.mybir as mybir

K, T, S, M, N = 1024, 2048, 1024, 512, 512
FLOPS = 2 * (2 * K * S * M + S * N * M + K * N * M)

F32 = mybir.dt.float32
BF16 = mybir.dt.bfloat16
I32 = mybir.dt.int32
U32 = mybir.dt.uint32
U16 = mybir.dt.uint16
U8 = mybir.dt.uint8
FP8X4 = mybir.dt.float8_e4m3fn_x4
FP4X4 = mybir.dt.float4_e2m1fn_x4
ACT = mybir.ActivationFunctionType
MULT = mybir.AluOpType.mult
ADD = mybir.AluOpType.add

P = 128
HALF = 256
CH = 128


def tile_list_divisive_norm_patch_kernel(
    tc, x, tab_words, tab_scales, tab2_words, tab2_scales, w4_words, w4_scales, wdT, g, offs, out
):
    nc = tc.nc
    with ExitStack() as ctx:
        keep = ctx.enter_context(tc.tile_pool(name="keep", bufs=1))
        psum = ctx.enter_context(tc.psum_pool(name="psum", bufs=1))

        def held(shape, dtype, name, tag=""):
            return keep.tile(shape, dtype, name=name, tag=tag or name, align_bytes=64)

        offsets = held([P, S // 16], U16, "offsets")
        nc.sync.dma_start(offsets[:], offs)

        def load_words(words, a, name):
            t = held([P, T], I32, name)
            nc.sync.dma_start(t[:], words[a].rearrange("p n t -> p (n t)").bitcast(I32))
            return t

        def zero_plane(width, name, engine):
            t = held([P, width], U8, name)
            engine.memset(t[:].bitcast(I32), 0)
            return t

        def load_table_scales(plane, scales):
            for q in range(4):
                nc.sync.dma_start(
                    plane[:].bitcast(I32)[32 * q : 32 * q + 8, :],
                    scales.bitcast(I32)[:, 4 * q : 4 * q + 4, :],
                )

        def load_x(h, a):
            t = held([P, 4, HALF], F32, "xraw%d%d" % (h, a))
            nc.sync.dma_start(
                t[:],
                x[512 * a : 512 * (a + 1), HALF * h : HALF * (h + 1)].rearrange("(p j) m -> p j m", j=4),
            )
            return t

        plane2 = held([P, T], U8, "plane2")
        nc.gpsimd.memset(plane2[:].bitcast(I32)[:, 0 : T // 8], 0)
        nc.vector.memset(plane2[:].bitcast(I32)[:, T // 8 : T // 4], 0)
        plane1 = zero_plane(T, "plane1", nc.vector)
        plane4 = zero_plane(2 * N, "plane4", nc.vector)
        warm = held([P, 2], F32, "warm")
        nc.vector.memset(warm[:, 0:1], 1.0)
        nc.scalar.activation(warm[:, 1:2], warm[:, 0:1], ACT.Abs_reciprocal_sqrt)
        grows = held([P, 2 * P], F32, "grows")
        nc.gpsimd.memset(grows[:], 0.0)
        nc.gpsimd.dma_start(
            grows[0:4, :].rearrange("t (q r) -> t q r", r=8),
            g.rearrange("(q t r) -> t q r", t=4, r=8),
        )
        ones = held([P, P], F32, "ones")
        nc.vector.memset(ones[:], 1.0)
        column = held([P, P], F32, "column")
        nc.vector.tensor_tensor_scan(column[:], ones[:], ones[:], -1.0, MULT, ADD)
        within = held([P, 32], F32, "within")
        nc.vector.transpose(within[:], column[:, 0:32])
        first = held([P, 1], F32, "first")
        for q in range(4):
            nc.vector.memset(first[32 * q : 32 * (q + 1), :], float(32 * q))
        ident = held([P, P], F32, "ident")
        row = held([P, 1], F32, "row")
        nc.gpsimd.tensor_tensor(row[:], first[:], within[:, 0:1], ADD)
        nc.gpsimd.tensor_scalar(ident[:], column[:], row[:], None, mybir.AluOpType.is_equal)

        for q in range(4):
            nc.gpsimd.dma_start(
                plane4[:].bitcast(I32)[32 * q : 32 * q + 4, :].rearrange("r (a n) -> r a n", a=2),
                w4_scales.bitcast(I32)[:, 4 * q : 4 * q + 4, :].rearrange("a r n -> r a n"),
            )
        words2, words1, xraw, wraw = [], [], {}, []
        w4 = held([P, 2, 2 * N], U8, "w4")

        def load_down(i):
            t = held([P, T], F32, "wraw%d" % i)
            nc.sync.dma_start(t[:], wdT[P * i : P * (i + 1), :])
            wraw.append(t)

        load_table_scales(plane2, tab2_scales)
        load_table_scales(plane1, tab_scales)
        words2.append(load_words(tab2_words, 0, "words2_0"))
        xraw[0, 0] = load_x(0, 0)
        xraw[0, 1] = load_x(0, 1)
        words2.append(load_words(tab2_words, 1, "words2_1"))
        xraw[1, 0] = load_x(1, 0)
        xraw[1, 1] = load_x(1, 1)
        words1.append(load_words(tab_words, 0, "words1_0"))
        words1.append(load_words(tab_words, 1, "words1_1"))
        load_down(0)
        load_down(1)
        nc.sync.dma_start(w4[:].bitcast(I32), w4_words.bitcast(I32).rearrange("a p c -> p a c"))
        load_down(2)
        load_down(3)

        def gather_words(window, b0, nb, name):
            t = held([P, 4, nb, P], U32, name)
            nc.vector.tensor_copy(
                t[:].rearrange("p t b (q r) -> p (b q) t r", r=8),
                window[:].bitcast(U32).indirect(offsets[:, 32 * b0 : 32 * (b0 + nb)]),
            )
            return [t[:, :, b, :] for b in range(nb)]

        def gather_scales(plane, name):
            picked = held([P, S], U8, name + "_picked")
            nc.vector.tensor_copy(picked[:], plane[:].indirect(offsets[:]))
            dealt = held([P, S], U8, name + "_dealt")
            nc.vector.tensor_copy(
                dealt[:].bitcast(I32).rearrange("p (b t q w) -> p b t q w", b=2, t=4, w=2),
                picked[:].bitcast(I32).rearrange("p (b q t w) -> p b t q w", b=2, t=4, w=2),
            )
            return dealt

        def quantize(src, width, name, tag=""):
            codes = held([P, width], U32, name + "_codes", tag)
            scales = held([P, width], U8, name + "_scales")
            nc.vector.quantize_mx(out=codes[:].bitcast(FP8X4), scales=scales[:], in_=src)
            return codes, scales

        def quantize_x(h):
            xg = held([P, 2, HALF, 4], BF16, "xg%d" % h)
            for a in range(2):
                nc.scalar.copy(
                    xg[:, a].rearrange("p (c i) t -> p c t i", i=4),
                    xraw[h, a][:].rearrange("p t (c i) -> p c t i", i=4),
                )
            return quantize(xg[:].rearrange("p a m t -> p (a m t)"), 2 * HALF, "xq%d" % h)

        def first_product(dst, picked, dealt, b, t, xq, m0, width):
            codes, scales = xq
            for a in range(2):
                cols = slice(HALF * a + m0, HALF * a + m0 + width)
                nc.tensor.matmul_mx(
                    out=dst,
                    lhsT=picked[a][b][:, t, :].bitcast(FP8X4),
                    lhsT_scale=dealt[4 * a : P, 512 * b + P * t : 512 * b + P * (t + 1)],
                    rhs=codes[:, cols].bitcast(FP8X4),
                    rhs_scale=scales[:, cols],
                    start=(a == 0),
                    stop=(a == 1),
                )

        dealt2 = gather_scales(plane2, "s2")
        dealt1 = gather_scales(plane1, "s1")
        picked2 = [gather_words(words2[0], 0, 2, "p2_0")]
        xq = [quantize_x(0)]
        picked2.append(gather_words(words2[1], 0, 1, "p2_10") + gather_words(words2[1], 1, 1, "p2_11"))
        xq.append(quantize_x(1))
        gcol = held([P, 8], F32, "gcol")
        picked1 = [gather_words(words1[a], 0, 2, "p1_%d" % a) for a in range(2)]
        picked_down = []
        for i in range(4):
            wb = held([P, S], BF16, "wb%d" % i)
            nc.vector.tensor_copy(
                wb[:].rearrange("p (u q r e) -> p q u e r", u=2, r=8, e=2),
                wraw[i][:].indirect(offsets[:]),
            )
            picked_down.append(wb)
        scratch = {}

        def squares(b, h):
            if (b, h) == (0, 0):
                sq = xraw[1, 1][:].rearrange("p j m -> p (j m)")
            else:
                sq = held([P, 4 * HALF], F32, "sq%d%d" % (b, h))
            for u in range(2):
                bank = psum.tile([P, 2, HALF], F32, name="bbank", tag="b", bufs=2)
                for e in range(2):
                    first_product(bank[:, e, :], picked2, dealt2, b, 2 * u + e, xq[h], 0, HALF)
                nc.scalar.activation(
                    sq[:, 2 * HALF * u : 2 * HALF * (u + 1)], bank[:].rearrange("p e m -> p (e m)"), ACT.Square
                )
            return sq

        def weights_of(b, h, square_root=True):
            sq = squared[b, h]
            root = held([P, 4 * HALF], F32, "root%d%d" % (b, h))
            nc.scalar.activation(root[:], sq[:, :], ACT.Abs_reciprocal_sqrt, bias=1.0)
            inv = None
            if square_root:
                inv = held([P, 4 * HALF], F32, "inv%d%d" % (b, h))
                nc.scalar.activation(inv[:], root[:], ACT.Square)
            scratch[b, h] = (sq, root, inv)

        def with_gain(b, h):
            inv = scratch[b, h][2]
            wg = held([P, 4, HALF], F32, "wg%d%d" % (b, h))
            for t in range(4):
                nc.scalar.activation(
                    wg[:, t, :], inv[:, HALF * t : HALF * (t + 1)], ACT.Copy, scale=gcol[:, 4 * b + t : 4 * b + t + 1]
                )
            return wg

        def responses(b, h, wg):
            hg = held([P, HALF, 4], BF16, "hg%d%d" % (b, h))
            for c in range(2):
                bank = psum.tile([P, 4, CH], F32, name="abank", tag="a", bufs=2)
                for t in range(4):
                    first_product(bank[:, t, :], picked1, dealt1, b, t, xq[h], CH * c, CH)
                nc.vector.tensor_tensor(
                    hg[:, CH * c : CH * (c + 1), :].rearrange("p (c i) t -> p c t i", i=4),
                    bank[:].rearrange("p t (c i) -> p c t i", i=4),
                    wg[:, :, CH * c : CH * (c + 1)].rearrange("p t (c i) -> p c t i", i=4),
                    MULT,
                )
            flat = hg[:].rearrange("p m t -> p (m t)")
            if (b, h) == (1, 1):
                parts = [quantize(flat[:, 4 * CH * c : 4 * CH * (c + 1)], CH, "hq11%d" % c) for c in range(2)]
                return [(codes[:, :], scales[:, :]) for codes, scales in parts]
            codes, scales = quantize(flat, HALF, "hq%d%d" % (b, h))
            return [(codes[:, CH * c : CH * (c + 1)], scales[:, CH * c : CH * (c + 1)]) for c in range(2)]

        def turn_gain():
            gbank = psum.tile([P, 2, P], F32, name="gbank", tag="b", bufs=2)
            for b in range(2):
                nc.tensor.transpose(gbank[:, b, :], grows[:, P * b : P * (b + 1)], ident[:])
            nc.scalar.copy(gcol[:].rearrange("p (b t) -> p b t", b=2), gbank[:, :, 0:4])

        def responses_aside(b, h):
            inv = scratch[b, h][2][:].rearrange("p (t m) -> p t m", t=4)
            drive = held([P, 4, HALF], F32, "drive%d%d" % (b, h))
            for u in range(2):
                bank = psum.tile([P, 2, HALF], F32, name="abank", tag="a", bufs=2)
                for e in range(2):
                    first_product(bank[:, e, :], picked1, dealt1, b, 2 * u + e, xq[h], 0, HALF)
                for e in range(2):
                    t = 2 * u + e
                    nc.scalar.activation(
                        drive[:, t, :], bank[:, e, :], ACT.Copy, scale=gcol[:, 4 * b + t : 4 * b + t + 1]
                    )
            hg = held([P, HALF, 4], BF16, "hg%d%d" % (b, h))
            for c in range(2):
                nc.gpsimd.tensor_tensor(
                    hg[:, CH * c : CH * (c + 1), :].rearrange("p (c i) t -> p c t i", i=4),
                    drive[:, :, CH * c : CH * (c + 1)].rearrange("p t (c i) -> p c t i", i=4),
                    inv[:, :, CH * c : CH * (c + 1)].rearrange("p t (c i) -> p c t i", i=4),
                    MULT,
                )
            return hg

        def responses_twice(b, h, engine):
            root = scratch[b, h][1][:].rearrange("p (t m) -> p t m", t=4)
            once = held([P, 4, HALF], F32, "once%d%d" % (b, h))
            for u in range(2):
                bank = psum.tile([P, 2, HALF], F32, name="abank", tag="a", bufs=2)
                for e in range(2):
                    first_product(bank[:, e, :], picked1, dealt1, b, 2 * u + e, xq[h], 0, HALF)
                for e in range(2):
                    t = 2 * u + e
                    nc.vector.scalar_tensor_tensor(
                        once[:, t, :], bank[:, e, :], gcol[:, 4 * b + t : 4 * b + t + 1], root[:, t, :], MULT, MULT
                    )
            hg = held([P, HALF, 4], BF16, "hg%d%d" % (b, h))
            for c in range(2):
                engine.tensor_tensor(
                    hg[:, CH * c : CH * (c + 1), :].rearrange("p (c i) t -> p c t i", i=4),
                    once[:, :, CH * c : CH * (c + 1)].rearrange("p t (c i) -> p c t i", i=4),
                    root[:, :, CH * c : CH * (c + 1)].rearrange("p t (c i) -> p c t i", i=4),
                    MULT,
                )
            return hg

        def quantize_h(hg, name, tag=""):
            codes, scales = quantize(hg[:].rearrange("p m t -> p (m t)"), HALF, name, tag)
            return [(codes[:, CH * c : CH * (c + 1)], scales[:, CH * c : CH * (c + 1)]) for c in range(2)]

        def down_weights(i, room):
            wb = picked_down[i]
            bank = psum.tile([P, 4, P], F32, name="wbank", tag="b" if i % 2 else "tr", bufs=2 if i % 2 else 1)
            for b in range(2):
                for u in range(2):
                    nc.tensor.transpose(
                        bank[:, 2 * b + u, :], wb[:].bitcast(F32)[:, 256 * u + P * b : 256 * u + P * (b + 1)], ident[:]
                    )
            words = room[:, 0 : 4 * P]
            nc.scalar.copy(
                words.rearrange("p (b n u) -> p b n u", b=2, u=2),
                bank[:].rearrange("p (b u) n -> p b n u", b=2),
            )
            return quantize(words.bitcast(BF16), 2 * P, "wq%d" % i)

        hq = {}
        wq = []
        squared = {(0, 0): squares(0, 0)}
        turn_gain()
        squared[1, 0] = squares(1, 0)
        weights_of(0, 0)
        hg00 = responses_aside(0, 0)
        squared[0, 1] = squares(0, 1)
        weights_of(1, 0)
        wq.append(down_weights(0, scratch[1, 0][0]))
        hg10 = responses_aside(1, 0)
        squared[1, 1] = squares(1, 1)
        weights_of(0, 1, True)
        hq[0, 0] = quantize_h(hg00, "hq00", "root01")
        wq.append(down_weights(1, scratch[0, 1][0]))
        hq[0, 1] = responses(0, 1, with_gain(0, 1))
        weights_of(1, 1)
        hq[1, 0] = quantize_h(hg10, "hq10", "root11")
        wq.append(down_weights(2, scratch[1, 1][0]))
        gained = with_gain(1, 1)
        wq.append(down_weights(3, scratch[1, 1][2]))
        hq[1, 1] = responses(1, 1, gained)

        out_view = out.rearrange("(i p) m -> p i m", p=P)
        for h in range(2):
            for c in range(2):
                last = (h, c) == (1, 1)
                bank = psum.tile([P, 4, CH], F32, name="obank", tag="b" if last else "o", bufs=2 if last else 3)
                xcodes, xscales = xq[h]
                for i in range(4):
                    for a in range(2):
                        cols = slice(HALF * a + CH * c, HALF * a + CH * (c + 1))
                        nc.tensor.matmul_mx(
                            out=bank[:, i, :],
                            lhsT=w4[:, a, 2 * P * i : 2 * P * (i + 1)].bitcast(FP4X4),
                            lhsT_scale=plane4[:, N * a + P * i : N * a + P * (i + 1)],
                            rhs=xcodes[:, cols].bitcast(FP8X4),
                            rhs_scale=xscales[:, cols],
                            start=(i == 0 and a == 0),
                            stop=False,
                        )
                order = [(b, i) for b in range(2) for i in range(4)]
                if h == 0:
                    order = [(b, i) for i in range(4) for b in range(2)]
                for b, i in order:
                    hcodes, hscales = hq[b, h][c]
                    wcodes, wscales = wq[i]
                    nc.tensor.matmul_mx(
                        out=bank[:, i, :],
                        lhsT=wcodes[:, P * b : P * (b + 1)].bitcast(FP8X4),
                        lhsT_scale=wscales[:, P * b : P * (b + 1)],
                        rhs=hcodes.bitcast(FP8X4),
                        rhs_scale=hscales,
                        start=False,
                        stop=(b == 1 and i == 3),
                    )
                res = held([P, 4, CH], F32, "res%d%d" % (h, c))
                if last:
                    nc.vector.tensor_copy(res[:], bank[:])
                else:
                    nc.scalar.copy(res[:], bank[:])
                m0 = HALF * h + CH * c
                nc.sync.dma_start(out_view[:, :, m0 : m0 + CH], res[:])
